import numpy as np, ml_dtypes
CORES = [4,20,60,84,92,100,116]
N = 7
KT, C = 8, 64
def setup_inputs(rng):
    return {"x": rng.standard_normal((N, 128, KT * C), dtype=np.float32).astype(ml_dtypes.bfloat16)}
def setup_inputs_big(rng):
    d = setup_inputs(rng)
    for k in ("x",): d[k] = (d[k].astype(np.float32) * 1024.0).astype(d[k].dtype)
    return d
def setup_inputs_small(rng):
    d = setup_inputs(rng)
    for k in ("x",): d[k] = (d[k].astype(np.float32) * (1 / 1024.0)).astype(d[k].dtype)
    return d
def setup_inputs_apart(rng):
    d = setup_inputs(rng)
    f = (10.0 ** rng.permutation(np.linspace(-1.5, 1.5, N))).astype(np.float32).reshape(N, 1, 1)
    for k in ("x",): d[k] = (d[k].astype(np.float32) * f).astype(d[k].dtype)
    return d
def reference(x):
    X = x.astype(np.float64)
    y = np.full((N, C, N * C), np.nan)
    for r in range(N):
        for i in range(N):
            s = i
            if s != r: y[r][:, C * i:C * i + C] = sum(X[r][:, C * t:C * t + C].T @ X[s][:, C * t:C * t + C] for t in range(KT))
    return {"y": y.astype(ml_dtypes.bfloat16 if x.dtype != np.float64 else np.float64)}

@@ -1,0 +1,260 @@
+from concourse.bass import DstId, RemoteDMATransfer
+
+N, KT, C = 7, 8, 64
+W = KT * C
+NCH = 1
+MAXCH = 4
+
+SCRATCH = {
+    "XH": ("sbuf", [128, W], "bfloat16"),
+    "XG": ("sbuf", [128, W], "bfloat16"),
+    "XL": ("sbuf", [128, W], "bfloat16"),
+    "AB": ("sbuf", [128, 2 * W], "bfloat16"),
+    "RW": ("sbuf", [128, 2 * C], "bfloat16"),
+    "R2": ("sbuf", [128, 2 * C], "bfloat16"),
+    "PS1": ("psum", [128, 512], "float32"),
+    "PS2": ("psum", [128, 512], "float32"),
+    "PS3": ("psum", [128, 512], "float32"),
+}
+for _L in range(N):
+    SCRATCH["ln%d" % _L] = ("sbuf", [128, 2 * C], "bfloat16")
+
+SEMAPHORES = (["ld%d" % k for k in range(MAXCH)]
+              + ["ax%d_%d" % (s, k) for s in range(N) for k in range(MAXCH)]
+              + ["m%s%d" % (kind, L) for kind in ("E", "1", "2") for L in range(N)]
+              + ["sent", "st", "vz", "abh", "abg", "pe1", "pe2", "pe3", "ve", "v1", "v2"])
+
+
+def _bits(m):
+    return [i for i in range(m.bit_length()) if (m >> i) & 1]
+
+
+def _sub(m, lo, n):
+    return sum(1 << i for i in _bits(m)[lo:lo + n])
+
+
+def _cnt(m):
+    return len(_bits(m))
+
+
+def _plan(cores, topo):
+    n = len(cores)
+    chip = [topo.chip(c) for c in cores]
+    first = [r for r in range(n) if r == 0 or topo.same_plane(chip[0], chip[r])]
+    second = [r for r in range(n) if r not in first]
+    big, small = (first, second) if len(first) >= len(second) else (second, first)
+    mated = [(o, e) for o in small for e in big if topo.mates(chip[o], chip[e])]
+    o2, es = mated[0] if mated else (small[1], big[2])
+    o1 = [r for r in small if r != o2][0]
+    a, b, c, d = [r for r in big if r != es]
+    allc = range(topo.CHIPS * topo.CORES_PER_CHIP)
+
+    def owners(r):
+        far = cores[small[0]] if r in big else cores[big[0]]
+        own = [k for k in allc if topo.chip(k) == chip[r] and k != cores[r] and topo.may_write(k, far)]
+        return sorted(own, key=lambda k: (topo.die(k) != topo.die(cores[r]), k))
+
+    own = [owners(r) for r in range(n)]
+    lines = [
+        (o2, o1, es, own[o2][0], True),
+        (a, b, o1, own[a][0], True),
+        (c, d, o1, own[d][0], True),
+        (a, c, o2, own[c][0], True),
+        (b, d, o2, own[b][0], True),
+        (es, a, d, cores[es], False),
+        (c, b, es, cores[c], False),
+    ]
+    ins = [[] for _ in range(n)]
+    offs = [[] for _ in range(n)]
+    relay = {}
+    used = [0] * n
+    for p, q, l, host, early in lines:
+        for m, buf in ((p, "XH"), (q, "XG"), (l, "XL")):
+            src = cores[m]
+            if host == src:
+                continue
+            if topo.chip(host) == chip[m]:
+                ins[m].append((host, buf))
+            elif topo.may_write(src, host):
+                offs[m].append((host, buf))
+            else:
+                rc = own[m][used[m]]
+                used[m] += 1
+                relay[rc] = (m, (host, buf))
+                if (rc, "XH") not in ins[m]:
+                    ins[m].append((rc, "XH"))
+    nch = [NCH if used[m] else 1 for m in range(n)]
+
+    xcnt = {}
+    calls = {}
+    for r in range(n):
+        src = cores[r]
+        offm = topo.mask(src, offs[r][0][0]) if offs[r] else 0
+        full = topo.mask(src, ins[r][0][0])
+        if len(ins[r]) == 2:
+            half = _cnt(full) // 2
+            rounds = [[([ins[r][0]], _sub(full, 0, half)), ([ins[r][1]], _sub(full, half, half))]]
+            if offs[r]:
+                rounds.append([(offs[r], offm)])
+        else:
+            rounds = [[([ins[r][0]], full & ~offm)] + ([(offs[r], offm)] if offs[r] else [])]
+        lst = []
+        for rnd in rounds:
+            for k in range(nch[r]):
+                lst.append(("ld%d" % k, 16, [("XH", r, k, dsts, m) for dsts, m in rnd]))
+            for dsts, m in rnd:
+                for x, _b in dsts:
+                    xcnt[(x, r)] = _cnt(m)
+        calls[src] = lst
+    for rc, (s, dst) in relay.items():
+        m = topo.mask(rc, dst[0])
+        calls[rc] = [("ax%d_%d" % (s, k), xcnt[(rc, s)], [("XH", s, k, [dst], m)]) for k in range(nch[s])]
+        xcnt[(dst[0], s)] = _cnt(m)
+
+    mm = []
+    for p, q, l, host, early in lines:
+        mk = topo.mask(host, cores[l])
+        for m in (p, q):
+            if cores[m] != host:
+                mk &= topo.mask(host, cores[m])
+        if early:
+            mm.append((mk, mk))
+        else:
+            h = _cnt(mk) // 2
+            mm.append((_sub(mk, 0, h), _sub(mk, h, h)))
+    return {"lines": lines, "nch": nch, "xcnt": xcnt, "calls": calls, "mm": mm}
+
+
+def rank_program(g, core, T, topo):
+    cores = list(T.cores)
+    P = _plan(cores, topo)
+    lines, nch, xcnt, mm = P["lines"], P["nch"], P["xcnt"], P["mm"]
+    rank = T.rank_of(core)
+    node = [L for L in range(len(lines)) if lines[L][3] == core]
+    if rank is None and core not in P["calls"] and not node:
+        return
+    sem = T.sem
+    sent = [0]
+
+    def did(x):
+        rid, pid, _s = topo.addr(x)
+        return DstId(rid=rid, pnc=pid)
+
+    def send(trs):
+        tl = []
+        for src, dsts, m, rs in trs:
+            tl.append(RemoteDMATransfer(dst_ids=[did(x) for x, _a in dsts], dma_engine_mask=m, remote_sem=rs,
+                                        srcs=[src], dsts=[ap for _x, ap in dsts], alu_op=0))
+            sent[0] += _cnt(m)
+        g.remote_dma_fused(tl, local_sem=sem.sent)
+
+    def xwaits(s):
+        if core == cores[s]:
+            return [(sem["ld%d" % k], 16) for k in range(nch[s])]
+        return [(sem["ax%d_%d" % (s, k)], xcnt[(core, s)]) for k in range(nch[s])]
+
+    def tiles(s, k):
+        per = KT // nch[s]
+        return range(k * per, (k + 1) * per)
+
+    if rank is not None:
+        w = W // nch[rank]
+        for k in range(nch[rank]):
+            q = g.sync if k % 2 == 0 else g.scalar
+            q.dma_start(T.XH[:, k * w:(k + 1) * w], T.x[:, k * w:(k + 1) * w]).then_inc(sem["ld%d" % k], 16)
+
+    for semn, cntv, trs in P["calls"].get(core, []):
+        g.wait_ge(sem[semn], cntv)
+        out = []
+        for buf, s, k, dsts, m in trs:
+            w = W // nch[s]
+            out.append((T[buf][:, k * w:(k + 1) * w], [(x, T[bn][:, k * w:(k + 1) * w]) for x, bn in dsts], m,
+                        sem["ax%d_%d" % (s, k)]))
+        send(out)
+
+    if node:
+        L = node[0]
+        p, q, l, host, early = lines[L]
+        v, te = g.vector, g.tensor
+        ln = T["ln%d" % L]
+        v.memset(T.R2[C:2 * C, :], 0).then_inc(sem.vz, 1)
+        for s, buf, off, sn in ((p, "XH", 0, "abh"), (q, "XG", C, "abg")):
+            for k, (ws, wc) in enumerate(xwaits(s)):
+                v.wait_ge(ws, wc)
+                for t in tiles(s, k):
+                    v.tensor_copy(T.AB[:, 2 * C * t + off:2 * C * t + off + C],
+                                  T[buf][:, C * t:C * t + C]).then_inc(sem[sn], 1)
+        te.wait_ge(sem.abh, KT)
+        te.wait_ge(sem.abg, KT)
+        for t in range(KT):
+            ab = T.AB[:, 2 * C * t:2 * C * (t + 1)]
+            te.matmul(T.PS3[:, 0:2 * C], ab, ab, start=(t == 0), stop=(t == KT - 1)).then_inc(sem.pe3, 1)
+        for k, (ws, wc) in enumerate(xwaits(l)):
+            te.wait_ge(ws, wc)
+            for t in tiles(l, k):
+                te.matmul(T.PS2[0:C, 0:2 * C], T.XL[:, C * t:C * t + C], T.AB[:, 2 * C * t:2 * C * (t + 1)],
+                          start=(t == 0), stop=(t == KT - 1)).then_inc(sem.pe2, 1)
+            for t in tiles(l, k):
+                te.matmul(T.PS1[:, 0:C], T.AB[:, 2 * C * t:2 * C * (t + 1)], T.XL[:, C * t:C * t + C],
+                          start=(t == 0), stop=(t == KT - 1)).then_inc(sem.pe1, 1)
+        v.wait_ge(sem.pe3, KT)
+        v.tensor_copy(T.RW[0:C, 0:C], T.PS3[0:C, C:2 * C]).then_inc(sem.ve, 1)
+        v.tensor_copy(T.RW[C:2 * C, 0:C], T.PS3[C:2 * C, 0:C]).then_inc(sem.ve, 1)
+        v.wait_ge(sem.pe2, KT)
+        v.tensor_copy(T.R2[0:C, :], T.PS2[0:C, 0:2 * C]).then_inc(sem.v2, 1)
+        v.wait_ge(sem.pe1, KT)
+        v.tensor_copy(T.RW[:, C:2 * C], T.PS1[:, 0:C]).then_inc(sem.v1, 1)
+
+        pq = [cores[m] for m in (p, q) if cores[m] != core]
+        mpq, ml = mm[L]
+        if early:
+            g.wait_ge(sem.ve, 2)
+            send([(T.RW[:, 0:C], [(x, ln[:, 0:C]) for x in pq], mpq, sem["mE%d" % L])])
+            g.wait_ge(sem.vz, 1)
+            g.wait_ge(sem.v2, 1)
+            send([(T.R2[:, :], [(cores[l], ln[:, :])], ml, sem["m2%d" % L])])
+            g.wait_ge(sem.v1, 1)
+            send([(T.RW[:, C:2 * C], [(x, ln[:, C:2 * C]) for x in pq], mpq, sem["m1%d" % L])])
+        else:
+            g.wait_ge(sem.ve, 2)
+            g.wait_ge(sem.vz, 1)
+            g.wait_ge(sem.v2, 1)
+            g.wait_ge(sem.v1, 1)
+            send([(T.RW[:, :], [(x, ln[:, :]) for x in pq], mpq, sem["m1%d" % L]),
+                  (T.R2[:, :], [(cores[l], ln[:, :])], ml, sem["m2%d" % L])])
+
+    nst = 0
+    if rank is not None:
+        stores = []
+        for L, (p, q, l, host, early) in enumerate(lines):
+            ln = T["ln%d" % L]
+            mpq, ml = mm[L]
+            late = 2 if early else 1
+            if rank in (p, q):
+                other = q if rank == p else p
+                if host == core:
+                    stores.append((late, sem.ve, 2, T.RW[0:C, 0:C], other, 1))
+                    stores.append((late, sem.v1, 1, T.RW[0:C, C:2 * C], l, 1))
+                else:
+                    r0 = 0 if rank == p else C
+                    s0 = sem["mE%d" % L] if early else sem["m1%d" % L]
+                    stores.append((0 if early else late, s0, _cnt(mpq), ln[r0:r0 + C, 0:C], other, 1))
+                    stores.append((late, sem["m1%d" % L], _cnt(mpq), ln[r0:r0 + C, C:2 * C], l, 1))
+            elif rank == l:
+                s2 = sem["m2%d" % L]
+                if q == p + 1:
+                    stores.append((late, s2, _cnt(ml), ln[0:C, :], p, 2))
+                else:
+                    stores.append((late, s2, _cnt(ml), ln[0:C, 0:C], p, 1))
+                    stores.append((late, s2, _cnt(ml), ln[0:C, C:2 * C], q, 1))
+        stores.sort(key=lambda e: e[0])
+        for i, (_o, ws, wc, src, blk, nb) in enumerate(stores):
+            qd = g.sync if i % 2 == 0 else g.scalar
+            qd.wait_ge(ws, wc)
+            qd.dma_start(T.y[:, C * blk:C * (blk + nb)], src).then_inc(sem.st, 16)
+            nst += 1
+
+    if sent[0]:
+        g.wait_ge(sem.sent, sent[0])
+    if nst:
+        g.wait_ge(sem.st, 16 * nst)

@@ -2,8 +2,9 @@ from concourse.bass import DstId, RemoteDMATransfer
 
 N, KT, C = 7, 8, 64
 W = KT * C
-NCH = 1
+NCH = 2
 MAXCH = 4
+NL = 5
 
 SCRATCH = {
     "XH": ("sbuf", [128, W], "bfloat16"),
@@ -12,16 +13,18 @@ SCRATCH = {
     "AB": ("sbuf", [128, 2 * W], "bfloat16"),
     "RW": ("sbuf", [128, 2 * C], "bfloat16"),
     "R2": ("sbuf", [128, 2 * C], "bfloat16"),
-    "PS1": ("psum", [128, 512], "float32"),
-    "PS2": ("psum", [128, 512], "float32"),
-    "PS3": ("psum", [128, 512], "float32"),
+    "lq": ("sbuf", [128, N * C], "bfloat16"),
 }
-for _L in range(N):
+for _i in range(1, 5):
+    SCRATCH["PS%d" % _i] = ("psum", [128, 512], "float32")
+for _L in range(NL):
     SCRATCH["ln%d" % _L] = ("sbuf", [128, 2 * C], "bfloat16")
 
 SEMAPHORES = (["ld%d" % k for k in range(MAXCH)]
               + ["ax%d_%d" % (s, k) for s in range(N) for k in range(MAXCH)]
-              + ["m%s%d" % (kind, L) for kind in ("E", "1", "2") for L in range(N)]
+              + ["m%s%d" % (kind, L) for kind in ("E", "1", "2") for L in range(NL)]
+              + ["mq%d" % s for s in range(N)]
+              + ["pm0", "pl0", "pm1", "pl1", "vm0", "vl0", "vm1", "vl1"]
               + ["sent", "st", "vz", "abh", "abg", "pe1", "pe2", "pe3", "ve", "v1", "v2"])
 
 
@@ -56,26 +59,23 @@ def _plan(cores, topo):
 
     own = [owners(r) for r in range(n)]
     lines = [
-        (o2, o1, es, own[o2][0], True),
-        (a, b, o1, own[a][0], True),
-        (c, d, o1, own[d][0], True),
-        (a, c, o2, own[c][0], True),
-        (b, d, o2, own[b][0], True),
-        (es, a, d, cores[es], False),
-        (c, b, es, cores[c], False),
+        (o2, o1, es, own[o2][0]),
+        (a, b, o1, own[a][0]),
+        (c, d, o1, own[d][0]),
+        (a, c, o2, own[c][0]),
+        (b, d, o2, own[b][0]),
     ]
+    pairs = [(a, es), (d, a), (es, d), (b, es), (c, b), (es, c)]
+    jobs = [[s for h, s in pairs if h == r] for r in range(n)]
     ins = [[] for _ in range(n)]
     offs = [[] for _ in range(n)]
     relay = {}
     used = [0] * n
-    for p, q, l, host, early in lines:
+    for p, q, l, host in lines:
         for m, buf in ((p, "XH"), (q, "XG"), (l, "XL")):
-            src = cores[m]
-            if host == src:
-                continue
             if topo.chip(host) == chip[m]:
                 ins[m].append((host, buf))
-            elif topo.may_write(src, host):
+            elif topo.may_write(cores[m], host):
                 offs[m].append((host, buf))
             else:
                 rc = own[m][used[m]]
@@ -83,6 +83,9 @@ def _plan(cores, topo):
                 relay[rc] = (m, (host, buf))
                 if (rc, "XH") not in ins[m]:
                     ins[m].append((rc, "XH"))
+    for r in range(n):
+        for j, s in enumerate(jobs[r]):
+            offs[s].append((cores[r], ("XG", "XL")[j]))
     nch = [NCH if used[m] else 1 for m in range(n)]
 
     xcnt = {}
@@ -112,17 +115,10 @@ def _plan(cores, topo):
         xcnt[(dst[0], s)] = _cnt(m)
 
     mm = []
-    for p, q, l, host, early in lines:
-        mk = topo.mask(host, cores[l])
-        for m in (p, q):
-            if cores[m] != host:
-                mk &= topo.mask(host, cores[m])
-        if early:
-            mm.append((mk, mk))
-        else:
-            h = _cnt(mk) // 2
-            mm.append((_sub(mk, 0, h), _sub(mk, h, h)))
-    return {"lines": lines, "nch": nch, "xcnt": xcnt, "calls": calls, "mm": mm}
+    for p, q, l, host in lines:
+        mk = topo.mask(host, cores[l]) & topo.mask(host, cores[p]) & topo.mask(host, cores[q])
+        mm.append(mk)
+    return {"lines": lines, "jobs": jobs, "pairs": pairs, "nch": nch, "xcnt": xcnt, "calls": calls, "mm": mm}
 
 
 def rank_program(g, core, T, topo):
@@ -134,6 +130,7 @@ def rank_program(g, core, T, topo):
     if rank is None and core not in P["calls"] and not node:
         return
     sem = T.sem
+    v, te = g.vector, g.tensor
     sent = [0]
 
     def did(x):
@@ -157,6 +154,9 @@ def rank_program(g, core, T, topo):
         per = KT // nch[s]
         return range(k * per, (k + 1) * per)
 
+    def tl_(buf, t):
+        return T[buf][:, C * t:C * t + C]
+
     if rank is not None:
         w = W // nch[rank]
         for k in range(nch[rank]):
@@ -174,16 +174,14 @@ def rank_program(g, core, T, topo):
 
     if node:
         L = node[0]
-        p, q, l, host, early = lines[L]
-        v, te = g.vector, g.tensor
+        p, q, l, host = lines[L]
         ln = T["ln%d" % L]
         v.memset(T.R2[C:2 * C, :], 0).then_inc(sem.vz, 1)
         for s, buf, off, sn in ((p, "XH", 0, "abh"), (q, "XG", C, "abg")):
             for k, (ws, wc) in enumerate(xwaits(s)):
                 v.wait_ge(ws, wc)
                 for t in tiles(s, k):
-                    v.tensor_copy(T.AB[:, 2 * C * t + off:2 * C * t + off + C],
-                                  T[buf][:, C * t:C * t + C]).then_inc(sem[sn], 1)
+                    v.tensor_copy(T.AB[:, 2 * C * t + off:2 * C * t + off + C], tl_(buf, t)).then_inc(sem[sn], 1)
         te.wait_ge(sem.abh, KT)
         te.wait_ge(sem.abg, KT)
         for t in range(KT):
@@ -192,10 +190,10 @@ def rank_program(g, core, T, topo):
         for k, (ws, wc) in enumerate(xwaits(l)):
             te.wait_ge(ws, wc)
             for t in tiles(l, k):
-                te.matmul(T.PS2[0:C, 0:2 * C], T.XL[:, C * t:C * t + C], T.AB[:, 2 * C * t:2 * C * (t + 1)],
+                te.matmul(T.PS2[0:C, 0:2 * C], tl_("XL", t), T.AB[:, 2 * C * t:2 * C * (t + 1)],
                           start=(t == 0), stop=(t == KT - 1)).then_inc(sem.pe2, 1)
             for t in tiles(l, k):
-                te.matmul(T.PS1[:, 0:C], T.AB[:, 2 * C * t:2 * C * (t + 1)], T.XL[:, C * t:C * t + C],
+                te.matmul(T.PS1[:, 0:C], T.AB[:, 2 * C * t:2 * C * (t + 1)], tl_("XL", t),
                           start=(t == 0), stop=(t == KT - 1)).then_inc(sem.pe1, 1)
         v.wait_ge(sem.pe3, KT)
         v.tensor_copy(T.RW[0:C, 0:C], T.PS3[0:C, C:2 * C]).then_inc(sem.ve, 1)
@@ -205,48 +203,63 @@ def rank_program(g, core, T, topo):
         v.wait_ge(sem.pe1, KT)
         v.tensor_copy(T.RW[:, C:2 * C], T.PS1[:, 0:C]).then_inc(sem.v1, 1)
 
-        pq = [cores[m] for m in (p, q) if cores[m] != core]
-        mpq, ml = mm[L]
-        if early:
-            g.wait_ge(sem.ve, 2)
-            send([(T.RW[:, 0:C], [(x, ln[:, 0:C]) for x in pq], mpq, sem["mE%d" % L])])
-            g.wait_ge(sem.vz, 1)
-            g.wait_ge(sem.v2, 1)
-            send([(T.R2[:, :], [(cores[l], ln[:, :])], ml, sem["m2%d" % L])])
-            g.wait_ge(sem.v1, 1)
-            send([(T.RW[:, C:2 * C], [(x, ln[:, C:2 * C]) for x in pq], mpq, sem["m1%d" % L])])
-        else:
-            g.wait_ge(sem.ve, 2)
-            g.wait_ge(sem.vz, 1)
-            g.wait_ge(sem.v2, 1)
-            g.wait_ge(sem.v1, 1)
-            send([(T.RW[:, :], [(x, ln[:, :]) for x in pq], mpq, sem["m1%d" % L]),
-                  (T.R2[:, :], [(cores[l], ln[:, :])], ml, sem["m2%d" % L])])
+        pq = [cores[p], cores[q]]
+        g.wait_ge(sem.ve, 2)
+        send([(T.RW[:, 0:C], [(x, ln[:, 0:C]) for x in pq], mm[L], sem["mE%d" % L])])
+        g.wait_ge(sem.vz, 1)
+        g.wait_ge(sem.v2, 1)
+        send([(T.R2[:, :], [(cores[l], ln[:, :])], mm[L], sem["m2%d" % L])])
+        g.wait_ge(sem.v1, 1)
+        send([(T.RW[:, C:2 * C], [(x, ln[:, C:2 * C]) for x in pq], mm[L], sem["m1%d" % L])])
+
+    myjobs = P["jobs"][rank] if rank is not None else []
+    if myjobs:
+        v.memset(T.R2[C:2 * C, 0:C * len(myjobs)], 0).then_inc(sem.vz, 1)
+        for ws, wc in xwaits(rank):
+            te.wait_ge(ws, wc)
+        for j, s in enumerate(myjobs):
+            buf = ("XG", "XL")[j]
+            for ws, wc in xwaits(s):
+                te.wait_ge(ws, wc)
+            for t in range(KT):
+                te.matmul(T["PS%d" % (2 * j + 1)][0:C, 0:C], tl_(buf, t), tl_("XH", t),
+                          start=(t == 0), stop=(t == KT - 1)).then_inc(sem["pm%d" % j], 1)
+            for t in range(KT):
+                te.matmul(T["PS%d" % (2 * j + 2)][0:C, 0:C], tl_("XH", t), tl_(buf, t),
+                          start=(t == 0), stop=(t == KT - 1)).then_inc(sem["pl%d" % j], 1)
+            v.wait_ge(sem["pm%d" % j], KT)
+            v.tensor_copy(T.R2[0:C, C * j:C * j + C], T["PS%d" % (2 * j + 1)][0:C, 0:C]).then_inc(sem["vm%d" % j], 1)
+            v.wait_ge(sem["pl%d" % j], KT)
+            v.tensor_copy(T.RW[0:C, C * j:C * j + C], T["PS%d" % (2 * j + 2)][0:C, 0:C]).then_inc(sem["vl%d" % j], 1)
+        g.wait_ge(sem.vz, 1)
+        for j, s in enumerate(myjobs):
+            g.wait_ge(sem["vm%d" % j], 1)
+            send([(T.R2[:, C * j:C * j + C], [(cores[s], T.lq[:, C * rank:C * rank + C])],
+                   topo.mask(core, cores[s]), sem["mq%d" % rank])])
 
     nst = 0
     if rank is not None:
         stores = []
-        for L, (p, q, l, host, early) in enumerate(lines):
+        for j, s in enumerate(myjobs):
+            stores.append((1, sem["vl%d" % j], 1, T.RW[0:C, C * j:C * j + C], s, 1))
+        for h, s in P["pairs"]:
+            if s == rank:
+                stores.append((1, sem["mq%d" % h], _cnt(topo.mask(cores[h], core)), T.lq[0:C, C * h:C * h + C], h, 1))
+        for L, (p, q, l, host) in enumerate(lines):
             ln = T["ln%d" % L]
-            mpq, ml = mm[L]
-            late = 2 if early else 1
+            nm = _cnt(mm[L])
             if rank in (p, q):
                 other = q if rank == p else p
-                if host == core:
-                    stores.append((late, sem.ve, 2, T.RW[0:C, 0:C], other, 1))
-                    stores.append((late, sem.v1, 1, T.RW[0:C, C:2 * C], l, 1))
-                else:
-                    r0 = 0 if rank == p else C
-                    s0 = sem["mE%d" % L] if early else sem["m1%d" % L]
-                    stores.append((0 if early else late, s0, _cnt(mpq), ln[r0:r0 + C, 0:C], other, 1))
-                    stores.append((late, sem["m1%d" % L], _cnt(mpq), ln[r0:r0 + C, C:2 * C], l, 1))
+                r0 = 0 if rank == p else C
+                stores.append((0, sem["mE%d" % L], nm, ln[r0:r0 + C, 0:C], other, 1))
+                stores.append((2, sem["m1%d" % L], nm, ln[r0:r0 + C, C:2 * C], l, 1))
             elif rank == l:
                 s2 = sem["m2%d" % L]
                 if q == p + 1:
-                    stores.append((late, s2, _cnt(ml), ln[0:C, :], p, 2))
+                    stores.append((2, s2, nm, ln[0:C, :], p, 2))
                 else:
-                    stores.append((late, s2, _cnt(ml), ln[0:C, 0:C], p, 1))
-                    stores.append((late, s2, _cnt(ml), ln[0:C, C:2 * C], q, 1))
+                    stores.append((2, s2, nm, ln[0:C, 0:C], p, 1))
+                    stores.append((2, s2, nm, ln[0:C, C:2 * C], q, 1))
         stores.sort(key=lambda e: e[0])
         for i, (_o, ws, wc, src, blk, nb) in enumerate(stores):
             qd = g.sync if i % 2 == 0 else g.scalar

@@ -2,30 +2,27 @@ from concourse.bass import DstId, RemoteDMATransfer
 
 N, KT, C = 7, 8, 64
 W = KT * C
-NCH = 2
-MAXCH = 4
-NL = 5
+NH = 2
+HW_ = W // NH
+TPH = KT // NH
+NB = 8
 
 SCRATCH = {
     "XH": ("sbuf", [128, W], "bfloat16"),
-    "XG": ("sbuf", [128, W], "bfloat16"),
-    "XL": ("sbuf", [128, W], "bfloat16"),
-    "AB": ("sbuf", [128, 2 * W], "bfloat16"),
-    "RW": ("sbuf", [128, 2 * C], "bfloat16"),
+    "YB": ("sbuf", [128, N * C], "bfloat16"),
     "R2": ("sbuf", [128, 2 * C], "bfloat16"),
     "lq": ("sbuf", [128, N * C], "bfloat16"),
 }
-for _i in range(1, 5):
+for _s in range(N):
+    SCRATCH["X%d" % _s] = ("sbuf", [128, W], "bfloat16")
+for _i in range(NB):
     SCRATCH["PS%d" % _i] = ("psum", [128, 512], "float32")
-for _L in range(NL):
-    SCRATCH["ln%d" % _L] = ("sbuf", [128, 2 * C], "bfloat16")
 
-SEMAPHORES = (["ld%d" % k for k in range(MAXCH)]
-              + ["ax%d_%d" % (s, k) for s in range(N) for k in range(MAXCH)]
-              + ["m%s%d" % (kind, L) for kind in ("E", "1", "2") for L in range(NL)]
+SEMAPHORES = (["ld%d" % k for k in range(NH)]
+              + ["ax%d_%d" % (s, k) for s in range(N) for k in range(NH)]
               + ["mq%d" % s for s in range(N)]
-              + ["pm0", "pl0", "pm1", "pl1", "vm0", "vl0", "vm1", "vl1"]
-              + ["sent", "st", "vz", "abh", "abg", "pe1", "pe2", "pe3", "ve", "v1", "v2"])
+              + ["pe%d" % b for b in range(NB)] + ["vc%d" % b for b in range(NB)]
+              + ["sent", "st", "vz"])
 
 
 def _bits(m):
@@ -46,88 +43,63 @@ def _plan(cores, topo):
     first = [r for r in range(n) if r == 0 or topo.same_plane(chip[0], chip[r])]
     second = [r for r in range(n) if r not in first]
     big, small = (first, second) if len(first) >= len(second) else (second, first)
-    mated = [(o, e) for o in small for e in big if topo.mates(chip[o], chip[e])]
-    o2, es = mated[0] if mated else (small[1], big[2])
-    o1 = [r for r in small if r != o2][0]
-    a, b, c, d = [r for r in big if r != es]
+    mated = [o for o in small for e in big if topo.mates(chip[o], chip[e])]
     allc = range(topo.CHIPS * topo.CORES_PER_CHIP)
 
-    def owners(r):
-        far = cores[small[0]] if r in big else cores[big[0]]
-        own = [k for k in allc if topo.chip(k) == chip[r] and k != cores[r] and topo.may_write(k, far)]
-        return sorted(own, key=lambda k: (topo.die(k) != topo.die(cores[r]), k))
-
-    own = [owners(r) for r in range(n)]
-    lines = [
-        (o2, o1, es, own[o2][0]),
-        (a, b, o1, own[a][0]),
-        (c, d, o1, own[d][0]),
-        (a, c, o2, own[c][0]),
-        (b, d, o2, own[b][0]),
-    ]
-    pairs = [(a, es), (d, a), (es, d), (b, es), (c, b), (es, c)]
-    jobs = [[s for h, s in pairs if h == r] for r in range(n)]
-    ins = [[] for _ in range(n)]
+    jobs = [[] for _ in range(n)]
     offs = [[] for _ in range(n)]
+    nb = len(big)
+    for d in (1, 2):
+        for i in range(nb):
+            jobs[big[i]].append(big[(i + d) % nb])
+            offs[big[(i + d) % nb]].append(big[i])
+    hs = mated[0] if mated else small[-1]
+    for o in small:
+        if o != hs:
+            jobs[hs].append(o)
+            offs[o].append(hs)
+
     relay = {}
-    used = [0] * n
-    for p, q, l, host in lines:
-        for m, buf in ((p, "XH"), (q, "XG"), (l, "XL")):
-            if topo.chip(host) == chip[m]:
-                ins[m].append((host, buf))
-            elif topo.may_write(cores[m], host):
-                offs[m].append((host, buf))
-            else:
-                rc = own[m][used[m]]
-                used[m] += 1
-                relay[rc] = (m, (host, buf))
-                if (rc, "XH") not in ins[m]:
-                    ins[m].append((rc, "XH"))
-    for r in range(n):
-        for j, s in enumerate(jobs[r]):
-            offs[s].append((cores[r], ("XG", "XL")[j]))
-    nch = [NCH if used[m] else 1 for m in range(n)]
+    scat = [[] for _ in range(n)]
+    for mine, other in ((big, small), (small, big)):
+        for i, r in enumerate(mine):
+            own = [k for k in allc if topo.chip(k) == chip[r] and k != cores[r] and topo.may_write(k, cores[other[0]])]
+            dies = sorted({topo.die(k) for k in own}, key=lambda d: d != topo.die(cores[r]))
+            sh = (i * (2 if len(other) > 2 else 1)) % len(other)
+            tg = other[sh:] + other[:sh]
+            for h in range(NH):
+                grp = [k for k in own if topo.die(k) == dies[h % len(dies)]]
+                order = tg if h % 2 == 0 else tg[::-1]
+                nf = 1 if len(order) <= 2 else 2
+                cut = (len(order) + nf - 1) // nf
+                fw = []
+                for f in range(nf):
+                    relay[grp[f]] = (r, h, order[f * cut:(f + 1) * cut])
+                    fw.append(grp[f])
+                scat[r].append(fw)
 
-    xcnt = {}
-    calls = {}
+    smask = []
     for r in range(n):
-        src = cores[r]
-        offm = topo.mask(src, offs[r][0][0]) if offs[r] else 0
-        full = topo.mask(src, ins[r][0][0])
-        if len(ins[r]) == 2:
-            half = _cnt(full) // 2
-            rounds = [[([ins[r][0]], _sub(full, 0, half)), ([ins[r][1]], _sub(full, half, half))]]
-            if offs[r]:
-                rounds.append([(offs[r], offm)])
-        else:
-            rounds = [[([ins[r][0]], full & ~offm)] + ([(offs[r], offm)] if offs[r] else [])]
-        lst = []
-        for rnd in rounds:
-            for k in range(nch[r]):
-                lst.append(("ld%d" % k, 16, [("XH", r, k, dsts, m) for dsts, m in rnd]))
-            for dsts, m in rnd:
-                for x, _b in dsts:
-                    xcnt[(x, r)] = _cnt(m)
-        calls[src] = lst
-    for rc, (s, dst) in relay.items():
-        m = topo.mask(rc, dst[0])
-        calls[rc] = [("ax%d_%d" % (s, k), xcnt[(rc, s)], [("XH", s, k, [dst], m)]) for k in range(nch[s])]
-        xcnt[(dst[0], s)] = _cnt(m)
-
-    mm = []
-    for p, q, l, host in lines:
-        mk = topo.mask(host, cores[l]) & topo.mask(host, cores[p]) & topo.mask(host, cores[q])
-        mm.append(mk)
-    return {"lines": lines, "jobs": jobs, "pairs": pairs, "nch": nch, "xcnt": xcnt, "calls": calls, "mm": mm}
+        full = topo.mask(cores[r], scat[r][0][0])
+        if offs[r] and len(scat[r][0]) == 1:
+            full &= ~topo.mask(cores[r], cores[offs[r][0]])
+        per = _cnt(full) // NH
+        smask.append([_sub(full, h * per, per) for h in range(NH)])
+    fmask = {}
+    for k, (r, h, tgs) in relay.items():
+        m = topo.mask(k, cores[tgs[0]])
+        for t in tgs:
+            m &= topo.mask(k, cores[t])
+        fmask[k] = m
+    return {"jobs": jobs, "offs": offs, "relay": relay, "scat": scat, "smask": smask, "fmask": fmask}
 
 
 def rank_program(g, core, T, topo):
     cores = list(T.cores)
     P = _plan(cores, topo)
-    lines, nch, xcnt, mm = P["lines"], P["nch"], P["xcnt"], P["mm"]
+    relay, jobs, offs = P["relay"], P["jobs"], P["offs"]
     rank = T.rank_of(core)
-    node = [L for L in range(len(lines)) if lines[L][3] == core]
-    if rank is None and core not in P["calls"] and not node:
+    if rank is None and core not in relay:
         return
     sem = T.sem
     v, te = g.vector, g.tensor
@@ -145,129 +117,92 @@ def rank_program(g, core, T, topo):
             sent[0] += _cnt(m)
         g.remote_dma_fused(tl, local_sem=sem.sent)
 
-    def xwaits(s):
-        if core == cores[s]:
-            return [(sem["ld%d" % k], 16) for k in range(nch[s])]
-        return [(sem["ax%d_%d" % (s, k)], xcnt[(core, s)]) for k in range(nch[s])]
+    def half(buf, h):
+        return T[buf][:, h * HW_:(h + 1) * HW_]
 
-    def tiles(s, k):
-        per = KT // nch[s]
-        return range(k * per, (k + 1) * per)
-
-    def tl_(buf, t):
+    def tile(buf, t):
         return T[buf][:, C * t:C * t + C]
 
-    if rank is not None:
-        w = W // nch[rank]
-        for k in range(nch[rank]):
-            q = g.sync if k % 2 == 0 else g.scalar
-            q.dma_start(T.XH[:, k * w:(k + 1) * w], T.x[:, k * w:(k + 1) * w]).then_inc(sem["ld%d" % k], 16)
+    if rank is None:
+        s, h, tgs = relay[core]
+        xs = "X%d" % s
+        g.wait_ge(sem["ax%d_%d" % (s, h)], _cnt(P["smask"][s][h]))
+        send([(half(xs, h), [(cores[t], half(xs, h)) for t in tgs], P["fmask"][core], sem["ax%d_%d" % (s, h)])])
+        g.wait_ge(sem.sent, sent[0])
+        return
 
-    for semn, cntv, trs in P["calls"].get(core, []):
-        g.wait_ge(sem[semn], cntv)
-        out = []
-        for buf, s, k, dsts, m in trs:
-            w = W // nch[s]
-            out.append((T[buf][:, k * w:(k + 1) * w], [(x, T[bn][:, k * w:(k + 1) * w]) for x, bn in dsts], m,
-                        sem["ax%d_%d" % (s, k)]))
-        send(out)
+    me = "X%d" % rank
+    for h in range(NH):
+        q = g.sync if h % 2 == 0 else g.scalar
+        q.dma_start(half("XH", h), T.x[:, h * HW_:(h + 1) * HW_]).then_inc(sem["ld%d" % h], 16)
+    for h in range(NH):
+        g.wait_ge(sem["ld%d" % h], 16)
+    send([(half("XH", h), [(k, half(me, h)) for k in P["scat"][rank][h]], P["smask"][rank][h],
+           sem["ax%d_%d" % (rank, h)]) for h in range(NH)])
+    if offs[rank]:
+        send([(T.XH[:, :], [(cores[x], T[me][:, :]) for x in offs[rank]], topo.mask(core, cores[offs[rank][0]]),
+               sem["ax%d_0" % rank])])
 
-    if node:
-        L = node[0]
-        p, q, l, host = lines[L]
-        ln = T["ln%d" % L]
-        v.memset(T.R2[C:2 * C, :], 0).then_inc(sem.vz, 1)
-        for s, buf, off, sn in ((p, "XH", 0, "abh"), (q, "XG", C, "abg")):
-            for k, (ws, wc) in enumerate(xwaits(s)):
-                v.wait_ge(ws, wc)
-                for t in tiles(s, k):
-                    v.tensor_copy(T.AB[:, 2 * C * t + off:2 * C * t + off + C], tl_(buf, t)).then_inc(sem[sn], 1)
-        te.wait_ge(sem.abh, KT)
-        te.wait_ge(sem.abg, KT)
-        for t in range(KT):
-            ab = T.AB[:, 2 * C * t:2 * C * (t + 1)]
-            te.matmul(T.PS3[:, 0:2 * C], ab, ab, start=(t == 0), stop=(t == KT - 1)).then_inc(sem.pe3, 1)
-        for k, (ws, wc) in enumerate(xwaits(l)):
-            te.wait_ge(ws, wc)
-            for t in tiles(l, k):
-                te.matmul(T.PS2[0:C, 0:2 * C], tl_("XL", t), T.AB[:, 2 * C * t:2 * C * (t + 1)],
-                          start=(t == 0), stop=(t == KT - 1)).then_inc(sem.pe2, 1)
-            for t in tiles(l, k):
-                te.matmul(T.PS1[:, 0:C], T.AB[:, 2 * C * t:2 * C * (t + 1)], tl_("XL", t),
-                          start=(t == 0), stop=(t == KT - 1)).then_inc(sem.pe1, 1)
-        v.wait_ge(sem.pe3, KT)
-        v.tensor_copy(T.RW[0:C, 0:C], T.PS3[0:C, C:2 * C]).then_inc(sem.ve, 1)
-        v.tensor_copy(T.RW[C:2 * C, 0:C], T.PS3[C:2 * C, 0:C]).then_inc(sem.ve, 1)
-        v.wait_ge(sem.pe2, KT)
-        v.tensor_copy(T.R2[0:C, :], T.PS2[0:C, 0:2 * C]).then_inc(sem.v2, 1)
-        v.wait_ge(sem.pe1, KT)
-        v.tensor_copy(T.RW[:, C:2 * C], T.PS1[:, 0:C]).then_inc(sem.v1, 1)
-
-        pq = [cores[p], cores[q]]
-        g.wait_ge(sem.ve, 2)
-        send([(T.RW[:, 0:C], [(x, ln[:, 0:C]) for x in pq], mm[L], sem["mE%d" % L])])
-        g.wait_ge(sem.vz, 1)
-        g.wait_ge(sem.v2, 1)
-        send([(T.R2[:, :], [(cores[l], ln[:, :])], mm[L], sem["m2%d" % L])])
-        g.wait_ge(sem.v1, 1)
-        send([(T.RW[:, C:2 * C], [(x, ln[:, C:2 * C]) for x in pq], mm[L], sem["m1%d" % L])])
-
-    myjobs = P["jobs"][rank] if rank is not None else []
+    myjobs = jobs[rank]
     if myjobs:
         v.memset(T.R2[C:2 * C, 0:C * len(myjobs)], 0).then_inc(sem.vz, 1)
-        for ws, wc in xwaits(rank):
-            te.wait_ge(ws, wc)
-        for j, s in enumerate(myjobs):
-            buf = ("XG", "XL")[j]
-            for ws, wc in xwaits(s):
-                te.wait_ge(ws, wc)
-            for t in range(KT):
-                te.matmul(T["PS%d" % (2 * j + 1)][0:C, 0:C], tl_(buf, t), tl_("XH", t),
-                          start=(t == 0), stop=(t == KT - 1)).then_inc(sem["pm%d" % j], 1)
-            for t in range(KT):
-                te.matmul(T["PS%d" % (2 * j + 2)][0:C, 0:C], tl_("XH", t), tl_(buf, t),
-                          start=(t == 0), stop=(t == KT - 1)).then_inc(sem["pl%d" % j], 1)
-            v.wait_ge(sem["pm%d" % j], KT)
-            v.tensor_copy(T.R2[0:C, C * j:C * j + C], T["PS%d" % (2 * j + 1)][0:C, 0:C]).then_inc(sem["vm%d" % j], 1)
-            v.wait_ge(sem["pl%d" % j], KT)
-            v.tensor_copy(T.RW[0:C, C * j:C * j + C], T["PS%d" % (2 * j + 2)][0:C, 0:C]).then_inc(sem["vl%d" % j], 1)
+    for h in range(NH):
+        te.wait_ge(sem["ld%d" % h], 16)
+    bank = 0
+    stores = []
+    for j, s in enumerate(myjobs):
+        xs = "X%d" % s
+        te.wait_ge(sem["ax%d_0" % s], _cnt(topo.mask(cores[s], core)))
+        bp, bo = bank, bank + 1
+        bank += 2
+        for t in range(KT):
+            te.matmul(T["PS%d" % bp][0:C, 0:C], tile(xs, t), tile("XH", t),
+                      start=(t == 0), stop=(t == KT - 1)).then_inc(sem["pe%d" % bp], 1)
+        for t in range(KT):
+            te.matmul(T["PS%d" % bo][0:C, 0:C], tile("XH", t), tile(xs, t),
+                      start=(t == 0), stop=(t == KT - 1)).then_inc(sem["pe%d" % bo], 1)
+        v.wait_ge(sem["pe%d" % bp], KT)
+        v.tensor_copy(T.R2[0:C, C * j:C * j + C], T["PS%d" % bp][0:C, 0:C]).then_inc(sem["vc%d" % bp], 1)
+        v.wait_ge(sem["pe%d" % bo], KT)
+        v.tensor_copy(T.YB[0:C, C * s:C * s + C], T["PS%d" % bo][0:C, 0:C]).then_inc(sem["vc%d" % bo], 1)
+        stores.append((0, sem["vc%d" % bo], 1, T.YB[0:C, C * s:C * s + C], s))
+
+    arr = []
+    for k, (s, h, tgs) in relay.items():
+        if rank in tgs:
+            arr.append((tgs.index(rank), h, s, _cnt(P["fmask"][k])))
+    arr.sort()
+    done, bk = {}, {}
+    for pos, h, s, cn in arr:
+        if s not in bk:
+            bk[s] = bank
+            bank += 1
+            done[s] = 0
+        b = bk[s]
+        te.wait_ge(sem["ax%d_%d" % (s, h)], cn)
+        for t in range(h * TPH, (h + 1) * TPH):
+            done[s] += 1
+            te.matmul(T["PS%d" % b][0:C, 0:C], tile("XH", t), tile("X%d" % s, t),
+                      start=(done[s] == 1), stop=(done[s] == KT)).then_inc(sem["pe%d" % b], 1)
+        if done[s] == KT:
+            v.wait_ge(sem["pe%d" % b], KT)
+            v.tensor_copy(T.YB[0:C, C * s:C * s + C], T["PS%d" % b][0:C, 0:C]).then_inc(sem["vc%d" % b], 1)
+            stores.append((2, sem["vc%d" % b], 1, T.YB[0:C, C * s:C * s + C], s))
+
+    if myjobs:
         g.wait_ge(sem.vz, 1)
-        for j, s in enumerate(myjobs):
-            g.wait_ge(sem["vm%d" % j], 1)
-            send([(T.R2[:, C * j:C * j + C], [(cores[s], T.lq[:, C * rank:C * rank + C])],
-                   topo.mask(core, cores[s]), sem["mq%d" % rank])])
+    for j, s in enumerate(myjobs):
+        g.wait_ge(sem["vc%d" % (2 * j)], 1)
+        send([(T.R2[:, C * j:C * j + C], [(cores[s], T.lq[:, C * rank:C * rank + C])],
+               topo.mask(core, cores[s]), sem["mq%d" % rank])])
 
-    nst = 0
-    if rank is not None:
-        stores = []
-        for j, s in enumerate(myjobs):
-            stores.append((1, sem["vl%d" % j], 1, T.RW[0:C, C * j:C * j + C], s, 1))
-        for h, s in P["pairs"]:
-            if s == rank:
-                stores.append((1, sem["mq%d" % h], _cnt(topo.mask(cores[h], core)), T.lq[0:C, C * h:C * h + C], h, 1))
-        for L, (p, q, l, host) in enumerate(lines):
-            ln = T["ln%d" % L]
-            nm = _cnt(mm[L])
-            if rank in (p, q):
-                other = q if rank == p else p
-                r0 = 0 if rank == p else C
-                stores.append((0, sem["mE%d" % L], nm, ln[r0:r0 + C, 0:C], other, 1))
-                stores.append((2, sem["m1%d" % L], nm, ln[r0:r0 + C, C:2 * C], l, 1))
-            elif rank == l:
-                s2 = sem["m2%d" % L]
-                if q == p + 1:
-                    stores.append((2, s2, nm, ln[0:C, :], p, 2))
-                else:
-                    stores.append((2, s2, nm, ln[0:C, 0:C], p, 1))
-                    stores.append((2, s2, nm, ln[0:C, C:2 * C], q, 1))
-        stores.sort(key=lambda e: e[0])
-        for i, (_o, ws, wc, src, blk, nb) in enumerate(stores):
-            qd = g.sync if i % 2 == 0 else g.scalar
-            qd.wait_ge(ws, wc)
-            qd.dma_start(T.y[:, C * blk:C * (blk + nb)], src).then_inc(sem.st, 16)
-            nst += 1
+    for hst in offs[rank]:
+        stores.append((1, sem["mq%d" % hst], _cnt(topo.mask(cores[hst], core)), T.lq[0:C, C * hst:C * hst + C], hst))
+    stores.sort(key=lambda e: e[0])
+    for i, (_o, ws, wc, src, blk) in enumerate(stores):
+        qd = g.sync if i % 2 == 0 else g.scalar
+        qd.wait_ge(ws, wc)
+        qd.dma_start(T.y[:, C * blk:C * (blk + 1)], src).then_inc(sem.st, 16)
 
-    if sent[0]:
-        g.wait_ge(sem.sent, sent[0])
-    if nst:
-        g.wait_ge(sem.st, 16 * nst)
+    g.wait_ge(sem.sent, sent[0])
+    g.wait_ge(sem.st, 16 * len(stores))

from concourse.bass import DstId, RemoteDMATransfer

N, KT, C = 7, 8, 64
W = KT * C
NH = 2
HW_ = W // NH
TPH = KT // NH
NB = 8

SCRATCH = {
    "XH": ("sbuf", [128, W], "bfloat16"),
    "YB": ("sbuf", [128, N * C], "bfloat16"),
    "R2": ("sbuf", [128, 2 * C], "bfloat16"),
    "lq": ("sbuf", [128, N * C], "bfloat16"),
}
for _s in range(N):
    SCRATCH["X%d" % _s] = ("sbuf", [128, W], "bfloat16")
for _i in range(NB):
    SCRATCH["PS%d" % _i] = ("psum", [128, 512], "float32")

SEMAPHORES = (["ld%d" % k for k in range(NH)]
              + ["ax%d_%d" % (s, k) for s in range(N) for k in range(NH)]
              + ["mq%d" % s for s in range(N)]
              + ["pe%d" % b for b in range(NB)] + ["vc%d" % b for b in range(NB)]
              + ["sent", "st", "vz"])


def _bits(m):
    return [i for i in range(m.bit_length()) if (m >> i) & 1]


def _sub(m, lo, n):
    return sum(1 << i for i in _bits(m)[lo:lo + n])


def _cnt(m):
    return len(_bits(m))


def _plan(cores, topo):
    n = len(cores)
    chip = [topo.chip(c) for c in cores]
    first = [r for r in range(n) if r == 0 or topo.same_plane(chip[0], chip[r])]
    second = [r for r in range(n) if r not in first]
    big, small = (first, second) if len(first) >= len(second) else (second, first)
    mated = [o for o in small for e in big if topo.mates(chip[o], chip[e])]
    allc = range(topo.CHIPS * topo.CORES_PER_CHIP)

    jobs = [[] for _ in range(n)]
    offs = [[] for _ in range(n)]
    nb = len(big)
    for d in (1, 2):
        for i in range(nb):
            jobs[big[i]].append(big[(i + d) % nb])
            offs[big[(i + d) % nb]].append(big[i])
    hs = mated[0] if mated else small[-1]
    for o in small:
        if o != hs:
            jobs[hs].append(o)
            offs[o].append(hs)

    relay = {}
    scat = [[] for _ in range(n)]
    for mine, other in ((big, small), (small, big)):
        for i, r in enumerate(mine):
            own = [k for k in allc if topo.chip(k) == chip[r] and k != cores[r] and topo.may_write(k, cores[other[0]])]
            dies = sorted({topo.die(k) for k in own}, key=lambda d: d != topo.die(cores[r]))
            sh = (i * (2 if len(other) > 2 else 1)) % len(other)
            tg = other[sh:] + other[:sh]
            for h in range(NH):
                grp = [k for k in own if topo.die(k) == dies[h % len(dies)]]
                order = tg if h % 2 == 0 else tg[::-1]
                nf = 1 if len(order) <= 2 else 2
                cut = (len(order) + nf - 1) // nf
                fw = []
                for f in range(nf):
                    relay[grp[f]] = (r, h, order[f * cut:(f + 1) * cut])
                    fw.append(grp[f])
                scat[r].append(fw)

    smask = []
    for r in range(n):
        full = topo.mask(cores[r], scat[r][0][0])
        if offs[r] and len(scat[r][0]) == 1:
            full &= ~topo.mask(cores[r], cores[offs[r][0]])
        per = _cnt(full) // NH
        smask.append([_sub(full, h * per, per) for h in range(NH)])
    fmask = {}
    for k, (r, h, tgs) in relay.items():
        m = topo.mask(k, cores[tgs[0]])
        for t in tgs:
            m &= topo.mask(k, cores[t])
        fmask[k] = m
    return {"jobs": jobs, "offs": offs, "relay": relay, "scat": scat, "smask": smask, "fmask": fmask}


def rank_program(g, core, T, topo):
    cores = list(T.cores)
    P = _plan(cores, topo)
    relay, jobs, offs = P["relay"], P["jobs"], P["offs"]
    rank = T.rank_of(core)
    if rank is None and core not in relay:
        return
    sem = T.sem
    v, te = g.vector, g.tensor
    sent = [0]

    def did(x):
        rid, pid, _s = topo.addr(x)
        return DstId(rid=rid, pnc=pid)

    def send(trs):
        tl = []
        for src, dsts, m, rs in trs:
            tl.append(RemoteDMATransfer(dst_ids=[did(x) for x, _a in dsts], dma_engine_mask=m, remote_sem=rs,
                                        srcs=[src], dsts=[ap for _x, ap in dsts], alu_op=0))
            sent[0] += _cnt(m)
        g.remote_dma_fused(tl, local_sem=sem.sent)

    def half(buf, h):
        return T[buf][:, h * HW_:(h + 1) * HW_]

    def tile(buf, t):
        return T[buf][:, C * t:C * t + C]

    if rank is None:
        s, h, tgs = relay[core]
        xs = "X%d" % s
        g.wait_ge(sem["ax%d_%d" % (s, h)], _cnt(P["smask"][s][h]))
        send([(half(xs, h), [(cores[t], half(xs, h)) for t in tgs], P["fmask"][core], sem["ax%d_%d" % (s, h)])])
        g.wait_ge(sem.sent, sent[0])
        return

    me = "X%d" % rank
    for h in range(NH):
        q = g.sync if h % 2 == 0 else g.scalar
        q.dma_start(half("XH", h), T.x[:, h * HW_:(h + 1) * HW_]).then_inc(sem["ld%d" % h], 16)
    for h in range(NH):
        g.wait_ge(sem["ld%d" % h], 16)
    send([(half("XH", h), [(k, half(me, h)) for k in P["scat"][rank][h]], P["smask"][rank][h],
           sem["ax%d_%d" % (rank, h)]) for h in range(NH)])
    if offs[rank]:
        send([(T.XH[:, :], [(cores[x], T[me][:, :]) for x in offs[rank]], topo.mask(core, cores[offs[rank][0]]),
               sem["ax%d_0" % rank])])

    myjobs = jobs[rank]
    if myjobs:
        v.memset(T.R2[C:2 * C, 0:C * len(myjobs)], 0).then_inc(sem.vz, 1)
    for h in range(NH):
        te.wait_ge(sem["ld%d" % h], 16)
    bank = 0
    stores = []
    for j, s in enumerate(myjobs):
        xs = "X%d" % s
        te.wait_ge(sem["ax%d_0" % s], _cnt(topo.mask(cores[s], core)))
        bp, bo = bank, bank + 1
        bank += 2
        for t in range(KT):
            te.matmul(T["PS%d" % bp][0:C, 0:C], tile(xs, t), tile("XH", t),
                      start=(t == 0), stop=(t == KT - 1)).then_inc(sem["pe%d" % bp], 1)
        for t in range(KT):
            te.matmul(T["PS%d" % bo][0:C, 0:C], tile("XH", t), tile(xs, t),
                      start=(t == 0), stop=(t == KT - 1)).then_inc(sem["pe%d" % bo], 1)
        v.wait_ge(sem["pe%d" % bp], KT)
        v.tensor_copy(T.R2[0:C, C * j:C * j + C], T["PS%d" % bp][0:C, 0:C]).then_inc(sem["vc%d" % bp], 1)
        v.wait_ge(sem["pe%d" % bo], KT)
        v.tensor_copy(T.YB[0:C, C * s:C * s + C], T["PS%d" % bo][0:C, 0:C]).then_inc(sem["vc%d" % bo], 1)
        stores.append((0, sem["vc%d" % bo], 1, T.YB[0:C, C * s:C * s + C], s))

    arr = []
    for k, (s, h, tgs) in relay.items():
        if rank in tgs:
            arr.append((tgs.index(rank), h, s, _cnt(P["fmask"][k])))
    arr.sort()
    done, bk = {}, {}
    for pos, h, s, cn in arr:
        if s not in bk:
            bk[s] = bank
            bank += 1
            done[s] = 0
        b = bk[s]
        te.wait_ge(sem["ax%d_%d" % (s, h)], cn)
        for t in range(h * TPH, (h + 1) * TPH):
            done[s] += 1
            te.matmul(T["PS%d" % b][0:C, 0:C], tile("XH", t), tile("X%d" % s, t),
                      start=(done[s] == 1), stop=(done[s] == KT)).then_inc(sem["pe%d" % b], 1)
        if done[s] == KT:
            v.wait_ge(sem["pe%d" % b], KT)
            v.tensor_copy(T.YB[0:C, C * s:C * s + C], T["PS%d" % b][0:C, 0:C]).then_inc(sem["vc%d" % b], 1)
            stores.append((2, sem["vc%d" % b], 1, T.YB[0:C, C * s:C * s + C], s))

    if myjobs:
        g.wait_ge(sem.vz, 1)
    for j, s in enumerate(myjobs):
        g.wait_ge(sem["vc%d" % (2 * j)], 1)
        send([(T.R2[:, C * j:C * j + C], [(cores[s], T.lq[:, C * rank:C * rank + C])],
               topo.mask(core, cores[s]), sem["mq%d" % rank])])

    for hst in offs[rank]:
        stores.append((1, sem["mq%d" % hst], _cnt(topo.mask(cores[hst], core)), T.lq[0:C, C * hst:C * hst + C], hst))
    stores.sort(key=lambda e: e[0])
    for i, (_o, ws, wc, src, blk) in enumerate(stores):
        qd = g.sync if i % 2 == 0 else g.scalar
        qd.wait_ge(ws, wc)
        qd.dma_start(T.y[:, C * blk:C * (blk + 1)], src).then_inc(sem.st, 16)

    g.wait_ge(sem.sent, sent[0])
    g.wait_ge(sem.st, 16 * len(stores))
